import numpy as np, ml_dtypes
CORES = [10,34,74,98]
N = 4
BF = ml_dtypes.bfloat16
def gentries(a):
    return np.ascontiguousarray(a.reshape(8, 16, -1).transpose(0, 2, 1)).reshape(8, -1)
def gtable(e):
    e = np.asarray(e); return np.ascontiguousarray(e.reshape(8, -1, 16).transpose(0, 2, 1)).reshape(128, -1).astype(np.int32)
W, K, RO, LG = 4096, 2, 3, 2
def turn(rng):
    o = np.argsort(rng.random((8, W)), axis=1); p = np.zeros((8, W), np.int64); h = W >> 1
    np.put_along_axis(p, o[:, :h], o[:, h:], 1); np.put_along_axis(p, o[:, h:], o[:, :h], 1)
    return p
def near(rng, p, noise):
    b = rng.integers(0, 256, (8, 16, W)); lo = np.minimum(np.arange(W)[None, :], p)
    b = np.take_along_axis(b, lo[:, None, :], 2)
    return np.clip(b[None] + rng.integers(-noise, noise + 1, (N, 8, 16, W)), 0, 255)
def pack(x, m):
    return {"fr": np.ascontiguousarray(x.reshape(N, 128, W)).astype(np.float32).astype(BF), "ptr": np.stack([gtable(a) for a in m])}
def setup_inputs(rng):
    p = turn(rng); x = near(rng, p, 6)
    x = np.where(rng.random((N, 8, 1, W)) < 0.25, rng.integers(0, 256, (N, 8, 16, W)), x)
    x = np.where(rng.random((8, 1, W)) < 0.06, rng.integers(0, 256, (8, 16, 1)), x)
    share = rng.choice(np.array([0.3, 0.5, 0.7]), (N, 8, 1))
    m = np.where(rng.random((N, 8, W)) < share, p[None], rng.integers(0, W, (N, 8, W)))
    return pack(x, m)
def setup_inputs_alike(rng):
    v = np.arange(W); h = (v + (W >> 1)) & (W - 1); x = near(rng, np.tile(h, (8, 1)), 5); m = np.zeros((N, 8, W), np.int64)
    for r in range(N):
        o = rng.permutation(8)
        for g in range(8):
            k = int(o[g])
            if k == 0:
                m[r, g] = 0; x[r ^ 1, g, :, 0] = 255; x[r ^ 1, g, :, 1] = 254
            elif k == 1: m[r, g] = W - 1
            elif k == 2: m[r, g] = v
            elif k == 3: m[r, g] = (v + 1) & (W - 1)
            elif k == 4: m[r, g] = W - 1 - v
            elif k == 5: m[r, g] = rng.choice(np.array([0, 3, W >> 1, W - 1]), W)
            else: m[r, g] = np.where(rng.random(W) < 0.7, h, rng.integers(0, W, W))
    return pack(x, m)
def setup_inputs_corners(rng):
    v = np.arange(W); L = W >> 5; low = np.arange(L); x = rng.integers(0, 256, (N, 8, 16, W)); m = np.zeros((N, 8, W), np.int64)
    role = np.zeros(N >> 1, np.int64); c0 = int(rng.integers(0, N >> 1)); role[c0 ^ 1] = 1; flip = int(rng.integers(0, 2))
    rest = [c for c in range(N >> 1) if c != c0 and c != c0 ^ 1]
    for i in range(len(rest)): role[rest[i]] = 2 + (i ^ flip)
    D = rng.integers(0, 32, 8); D[int(rng.integers(0, 8))] = 0; side = rng.integers(0, 2, 8); lone = int(rng.integers(0, 8))
    for c in range(N >> 1):
        k = int(role[c])
        for g in range(8):
            a = 2 * c + (int(side[g]) ^ int(k == 1)); b = a ^ 1
            if k == 2:
                m[a, g] = (v + g) & (W - 1); m[b, g] = (v + 1 + g) & (W - 1)
                x[a, g] = 255 * rng.integers(0, 2, (1, W))
                x[b, g] = np.where(rng.random((1, W)) < 0.5, 255 * rng.integers(0, 2, (1, W)), x[b, g])
                continue
            if k == 3 and g & 1 == 1:
                m[a, g] = 0; m[b, g] = W - 1 if g & 2 == 2 else v
                continue
            if k == 3: w = rng.permutation(W)
            else:
                kind = 1 if k == 1 and g == lone else int(rng.integers(0, 4))
                if kind == 0: lo = low
                elif kind == 1: lo = L - 1 - low
                elif kind == 2: lo = low ^ 1
                else: lo = np.argsort(rng.random((32, L)), axis=1)
                w = (((np.arange(32)[:, None] + int(D[g]) + 4 * int(k == 1)) & 31) * L + lo).reshape(-1)
            m[a, g] = w; m[b, g, w] = v
            x[b, g][:, w] = np.clip(x[a, g] + rng.integers(-7, 8, (16, W)), 0, 255)
            if k == 3: m[a, g] = np.where(rng.random(W) < 0.5, rng.integers(0, W, W), m[a, g])
            if k == 1 and g == lone:
                u = L * int(rng.integers(0, 32)) + int(rng.integers(2, L)); m[a, g, u] = int(w[u]) ^ 1
    return pack(x, m)
def setup_inputs_ends(rng):
    p = turn(rng); v = np.arange(W); lo = np.minimum(v[None, :], p)
    kind = rng.integers(0, 3, (8, 1, W)); b = 255 * np.where(kind == 2, rng.integers(0, 2, (8, 16, W)), kind)
    b = np.take_along_axis(b, lo[:, None, :], 2)
    x = np.where(rng.random((N, 8, 1, W)) < 0.25, 255 * rng.integers(0, 2, (N, 8, 16, W)), b[None])
    one = (rng.random((N, 8, 1, W)) < 0.25) & (np.arange(16)[:, None] == rng.integers(0, 16, (N, 8, 1, W)))
    x = np.where(one, np.abs(x - 1), x)
    u = rng.random((8, W)); hit = np.minimum(u, np.take_along_axis(u, p, 1)) < 0.15
    m = np.where(hit[None] & (rng.random((N, 8, W)) < 0.9), p[None], (W - 1) * rng.integers(0, 2, (N, 8, W)))
    for r in range(N):
        for g in range(8):
            s = (r ^ g) & 1
            if s == 1: m[r, g, 0] = W - 1; m[r, g, W - 1] = 0
            else: m[r, g, 0] = 0; m[r, g, W - 1] = W - 1
            m[r, g, W - 2] = W - 1
            for c in (0, 1, 2, 3, W - 2, W - 1): x[r, g, :, c] = 255 * s
            t = g >> 1
            if t > 0: x[r, g, int(rng.integers(0, 16)), (0, W - 1, 0, 1)[t]] = abs(255 * s - 1)
    return pack(x, m)
def setup_inputs_spread(rng):
    p = turn(rng); x = near(rng, p, 3); lo = np.minimum(np.arange(W)[None, :], p)
    sh = np.take_along_axis(rng.integers(0, 8, (8, W)), lo, 1)[None]
    sh = np.where(rng.random((N, 8, W)) < 0.3, rng.integers(0, 8, (N, 8, W)), sh)
    x = (x >> sh[:, :, None, :]) * (rng.random((N, 8, 1, W)) > 0.0625)
    w = np.minimum((W * rng.random((N, 8, W)) ** 4).astype(np.int64), W - 1)
    w = np.where(rng.random((N, 8, 1)) < 0.5, w, W - 1 - w)
    m = np.where(rng.random((N, 8, W)) < 0.4, p[None], w)
    return pack(x, m)
def setup_inputs_ties(rng):
    p = turn(rng); pal = rng.choice(np.array([0, 1, 100, 127, 128, 254, 255]), (8, 16, 4))
    pal[:, 0, 0] = 0; pal[:, 1, 0] = 200; pal[:, :, 1] = pal[:, :, 0]; pal[:, 0, 1] = 200; pal[:, 1, 1] = 0
    pal[:, 0:2, 2] = 128; pal[:, 0:2, 3] = 5
    ix = rng.integers(0, 4, (N, 8, W))
    x = np.take_along_axis(np.tile(pal[None], (N, 1, 1, 1)), ix[:, :, None, :], 3)
    x = np.where(rng.random((N, 8, 1, W)) < 0.125, rng.integers(0, 256, (N, 8, 16, W)), x)
    m = np.where(rng.random((N, 8, W)) < 0.5, p[None], rng.integers(0, W, (N, 8, W)))
    return pack(x, m)
def check_inputs(d):
    bad = []
    for k, lo, hi in (("fr", 0, 255), ("ptr", 0, W - 1)):
        a = np.asarray(d[k]).astype(np.float64)
        if not (np.min(a) >= lo and np.max(a) <= hi): bad.append("range of " + k)
        if not np.all(a == np.floor(a)): bad.append("whole numbers in " + k)
    return bad
def reference(fr, ptr):
    x = fr.astype(np.float32).astype(np.int32).reshape(N, 8, 16, W)
    m = np.stack([gentries(a) for a in ptr]).astype(np.int64)
    cnt = [0] * N; own = np.arange(W)[None, :]
    for t in range(RO):
        h = 1 << (t % LG); chosen = []
        for r in range(N):
            a, n, xq = m[r], m[r ^ h], x[r ^ h]
            es = [a]
            for i in range(K): es.append(np.take_along_axis(a, np.take_along_axis(n, es[-1], 1), 1))
            es.append((np.roll(a, 1, axis=1) + 1 + (cnt[r] & 3)) & (W - 1))
            far = np.stack([np.sum(np.abs(np.take_along_axis(xq, e[:, None, :], 2) - x[r]), axis=1) for e in es])
            first = np.argmin(far, axis=0)
            chosen.append(np.take_along_axis(np.stack(es), first[None], 0)[0])
        lifted = []
        for r in range(N):
            q = r ^ h
            con = np.take_along_axis(chosen[q], chosen[r], 1) == own
            c = con[:, None, :]; y = np.take_along_axis(x[q], chosen[r][:, None, :], 2)
            if r < q: lifted.append(np.where(c, (x[r] + y) >> 1, x[r]))
            else:
                z = np.abs(x[r] - y); lifted.append(np.where(c, z, z >> 1))
            cnt[r] = int(np.sum(con))
        x = np.stack(lifted); m = np.stack(chosen)
    return {"yf": x.reshape(N, 128, W).astype(np.float32).astype(BF), "yp": np.stack([gtable(a) for a in m]).astype(np.float32)}

import numpy as np
from concourse.bass import DstId, RemoteDMATransfer
from concourse.mybir import AluOpType as Alu, AxisListType as Ax, ActivationFunctionType as Act

W = 4096
HS = [1, 2, 1]
USE_HELPERS = True
YE = [["dve", "act", "dve", "act"], ["dve", "act", "dve", "act"], ["dve", "act", "dve", "act"]]
BE = [["act"] * 4, ["act"] * 4, ["act"] * 4]
CE = [["act"] * 4, ["act"] * 4, ["act"] * 4]
PE0 = ["act", "act"]
ORDER = [(0, 0), (3, 0), (0, 1), (1, 0), (2, 0), (3, 1), (1, 1), (2, 1)]
DCH = [1024, 1024]
DLAST = [1024, 640, 384]
KE = "dve"
TRIES = 40
SLACK = 130.0
NOISE = 300.0
BOOST = 3000.0
A2 = 16 + 4 * W
MAGIC = 12582912.0
BF, F32, I32, U16 = "bfloat16", "float32", "int32", "uint16"
MATS = ["P0", "P1", "P2", "P0x64", "P1d", "P2d", "S1", "S2", "S1d", "S2d", "R1", "R2", "R1d", "R2d", "I4096", "I16384",
        "In63", "In64", "Ih", "A0", "A1", "A2", "K0", "K2", "K3", "Kn", "K8", "B1", "B2", "CDG"]
COLS = ["p", "k", "s16", "b0", "b1", "x1", "x2", "x3", "t0", "t1", "t2", "t3", "odd", "r0", "r1", "r2", "r3", "wt", "a0", "a1", "a2",
        "y0", "y1", "y2", "m0", "m1", "sl", "u0", "u1", "u2", "u3", "nl", "la", "v0", "v1", "v2", "v3", "v4", "v5", "cx", "cc"]

SCRATCH = {
    "XW": ("sbuf", [128, W + 16], BF), "XS": ("sbuf", [128, W], BF), "DW": ("sbuf", [128, 16 + 8 * W], BF),
    "PW": ("sbuf", [128, W], BF), "GA": ("sbuf", [128, W], BF), "GB": ("sbuf", [128, W], BF), "GC": ("sbuf", [128, W], BF),
    "YG": ("sbuf", [128, W], BF), "SF": ("sbuf", [128, W], F32),
    "MT": ("sbuf", [128, 128 * len(MATS)], BF), "UK": ("sbuf", [128, 16 * 144], BF), "UB": ("sbuf", [128, 4 * 144], BF),
    "CW": ("sbuf", [128, 3 * 144], BF), "CS": ("sbuf", [128, 96], BF), "ONE": ("sbuf", [128, 256], BF),
    "JF": ("sbuf", [128, 256], F32), "JB": ("sbuf", [128, 256], BF), "JK": ("sbuf", [128, 256], BF), "M16": ("sbuf", [128, 16], F32),
    "CF": ("sbuf", [128, len(COLS)], F32), "CI": ("sbuf", [128, 8], I32),
    "PI": ("sbuf", [128, 256], I32), "XI": ("sbuf", [128, 768], I32), "KI": ("sbuf", [128, 512], I32), "KF": ("sbuf", [128, 512], F32),
    "TB": ("sbuf", [128, 768], BF), "HL": ("sbuf", [128, 544], BF), "CON": ("sbuf", [128, 256], BF), "FL": ("sbuf", [128, 256], BF),
    "LM": ("sbuf", [128, 256], U16), "LU": ("sbuf", [128, 256], U16), "L1": ("sbuf", [128, 256], U16), "L2": ("sbuf", [128, 256], U16),
    "L3": ("sbuf", [128, 256], U16), "LY": ("sbuf", [128, 256], U16), "YP": ("sbuf", [128, 256], F32),
    "CN0": ("sbuf", [128, 32], BF), "CN1": ("sbuf", [128, 32], BF),
    "PS": ("psum", [128, 4096], F32),
    "PST": ("dram", [4, 128, 64], I32), "PLD": ("dram", [4, 128, 64], I32),
    "FST": ("dram", [8, 128, 512], BF), "FLD": ("dram", [8, 128, 512], BF),
    "OST": ("dram", [16, 128, 256], BF), "OLD": ("dram", [16, 128, 256], BF),
    "QST": ("dram", [4, 128, 64], F32), "QLD": ("dram", [4, 128, 64], F32),
}
NDMA = 64
SEMAPHORES = (["dve", "act", "pe", "pool", "sent", "ap", "ay", "ac0", "ac1", "hf", "ho0", "ho2"] + ["af%d" % i for i in range(8)]
              + ["ao%d" % i for i in range(4)] + ["d%d" % i for i in range(NDMA)])

CYC, PEC, GATH, HOP = 1.0, 0.5, 1.56, 120.0


def helpers_of(T, topo):
    out = {}
    for r, c in enumerate(T.cores):
        free = [x for x in topo.cores_of(c) if topo.die(x) != topo.die(c) and T.rank_of(x) is None]
        dests = sorted([k for k in range(4) if k != r], key=lambda k: sum(topo.may_write(x, T.cores[k]) for x in free))
        for k in dests:
            ok = [x for x in free if topo.may_write(x, T.cores[k])]
            ok.sort(key=lambda x: sum(topo.may_write(x, d) for d in T.cores if d != c))
            out[(r, k)] = ok[0]
            free.remove(ok[0])
    return out


def bits(es):
    return sum(1 << e for e in es)


def helper_program(g, core, T, topo, r, k):
    src, dst = T.cores[r], T.cores[k]
    rid, pid, _ = topo.addr(dst)
    m = topo.mask(core, dst)
    n = len(topo.engines(core, dst))
    got = len(fan_engines(T, topo, r)[k])
    g.wait_ge(T.sem.hf, got)
    g.remote_dma(T.FLD[r], T.FLD[r], T.sem["af%d" % r], T.sem.sent, pid, rid, m)
    for c in (0, 2):
        g.wait_ge(T.sem["ho%d" % c], got)
        g.remote_dma(T.OLD[4 * c + r], T.OLD[4 * c + r], T.sem["ao%d" % c], T.sem.sent, pid, rid, m)
    g.wait_ge(T.sem.sent, 3 * n)


def split3(es, r):
    q = len(es) // 4
    parts = [es[:2 * q], es[2 * q:3 * q], es[3 * q:]]
    return {k: parts[i] for i, k in enumerate([k for k in range(4) if k != r])}


def fan_engines(T, topo, r):
    c = T.cores[r]
    off = topo.engines(c, T.cores[r ^ 1])
    mate = [x for x in topo.cores_of(c) if x != c][0]
    return split3([e for e in topo.engines(c, mate) if e not in off], r)


def rank_program(g, core, T, topo):
    me = T.rank_of(core)
    hp = helpers_of(T, topo)
    if me is None:
        if USE_HELPERS:
            for (r, k), x in hp.items():
                if x == core:
                    helper_program(g, core, T, topo, r, k)
        return
    ops = []
    others = [(me + i) % 4 for i in (1, 2, 3)]

    def V(name, lo, hi, step=1, p0=0, p1=128):
        return (T[name][p0:p1, lo:hi:step], name, lo, hi, p0, p1, step)

    def D(ap, name, lo, hi):
        return (ap, name, lo, hi, 0, 128, 1)

    def PS(bank, lo, hi, step=1):
        return V("PS", 512 * bank + lo, 512 * bank + hi, step)

    def M(name):
        i = MATS.index(name)
        return V("MT", 128 * i, 128 * i + 128)

    def C(name):
        i = COLS.index(name)
        return V("CF", i, i + 1)

    def add(eng, kind, reads, writes, fns, busy, lat=0.0, after=None, sem=None):
        ops.append({"eng": eng, "kind": kind, "r": [x[1:] for x in reads], "w": [x[1:] for x in writes], "fns": fns,
                    "busy": busy, "lat": lat, "after": after, "sem": sem})
        return len(ops) - 1

    last = {}

    def chain():
        e = ops[-1]["eng"]
        ops[-1]["behind"] = last.get(e)
        last[e] = len(ops) - 1

    def width(v):
        return int(v[0].shape[-1])

    def sc(x):
        return x[0] if isinstance(x, tuple) else x

    def tup(xs):
        return [x for x in xs if isinstance(x, tuple)]

    def ts(out, in0, s1, s2, op0, op1=None, half=False):
        if op1 is None:
            f = lambda: g.vector.tensor_scalar(out[0], in0[0], sc(s1), None, op0)
        else:
            f = lambda: g.vector.tensor_scalar(out[0], in0[0], sc(s1), sc(s2), op0, op1)
        add("dve", "c", [in0] + tup([s1, s2]), [out], [f], 50 + CYC * max(64, width(out) * (0.5 if half else 1)))

    def tt(out, in0, in1, op, f=1):
        add("dve", "c", [in0, in1], [out], [lambda: g.vector.tensor_tensor(out[0], in0[0], in1[0], op)], 50 + CYC * max(64, f * width(out)))

    def cp(out, in0):
        add("dve", "c", [in0], [out], [lambda: g.vector.tensor_copy(out[0], in0[0])], 50 + CYC * max(64, width(out)))

    def fill(out, c):
        add("dve", "c", [], [out], [lambda: g.vector.memset(out[0], c)], 50 + CYC * max(64, width(out) / 2))

    def act(out, in0, func=Act.Identity, scale=1.0):
        add("act", "c", [in0] + tup([scale]), [out], [lambda: g.scalar.activation(out[0], in0[0], func, scale=sc(scale))],
            65 + CYC * max(64, width(out)))

    def copy(eng, out, in0):
        if eng == "act":
            act(out, in0)
        else:
            cp(out, in0)

    def gather(eng, out, win, lst, lo, hi, sub=None):
        off = V(lst, lo // 16, hi // 16)
        src = lambda: win[0].indirect(off[0])
        if sub is not None:
            f = lambda: g.vector.tensor_tensor(out[0], src(), sub[0], Alu.subtract)
        elif eng == "act":
            f = lambda: g.scalar.activation(out[0], src(), Act.Identity)
        else:
            f = lambda: g.vector.tensor_copy(out[0], src())
        add(eng, "c", [win, off] + tup([sub]), [out], [f], 60 + CYC * GATH * (hi - lo))
        ops[-1]["gn"] = hi - lo

    def mm(items):
        fns = [(lambda o=o, l=l, r=r, a=a, b=b: g.tensor.matmul(o[0], l[0], r[0], a, b)) for o, l, r, a, b in items]
        add("pe", "c", [x[1] for x in items] + [x[2] for x in items], [x[0] for x in items], fns,
            30 + PEC * sum(max(64, width(x[2])) for x in items))

    def dma(q, pairs, nbytes):
        eng = {"sp": g.sync, "act": g.scalar}[q]
        fns = [(lambda o=o, i=i: eng.dma_start(o[0], i[0])) for o, i in pairs]
        return add(q, "d", [x[1] for x in pairs], [x[0] for x in pairs], fns, 60.0 * len(pairs), 2000 + nbytes / 150.0)

    nsent = [0]

    def send(items):
        def f():
            if len(items) == 1:
                c, d, s, sem, es = items[0]
                rid, pid, _ = topo.addr(c)
                return g.remote_dma(d, s[0], T.sem[sem], T.sem.sent, pid, rid, bits(es))
            return g.remote_dma_fused([RemoteDMATransfer(dst_ids=[DstId(rid=topo.addr(c)[0], pnc=topo.addr(c)[1])], dma_engine_mask=bits(es),
                                                         remote_sem=T.sem[sem], src=s[0], dst=d) for c, d, s, sem, es in items],
                                      local_sem=T.sem.sent)
        nsent[0] += sum(len(x[4]) for x in items)
        return add("pool", "r", [x[2] for x in items], [], [f], 600.0)

    def arrive(sem, count, writes, after, lat):
        add(None, "a", [], writes, [], 0.0, lat, after, (sem, count))

    def off_engines(r, k):
        return topo.engines(T.cores[r], T.cores[k])

    def small(r):
        return split3(off_engines(r, r ^ 1), r)

    dma("sp", [(D(T.PST[:], "PST", 0, 4), D(T.ptr[:], "ptr", 0, 1))], 131072)
    dma("act", [(D(T.FST[0:4], "FST", 0, 4), D(T.fr[:, 0:2048], "fr", 0, 1))], 524288)
    dma("sp", [(D(T.FST[4:8], "FST", 4, 8), D(T.fr[:, 2048:W], "fr", 0, 1))], 900000)
    dma("sp", [(V("PI", 0, 256, 1, 32 * me, 32 * me + 32), D(T.ptr[32 * me:32 * me + 32, :], "ptr", 0, 1))], 32768)
    add("pool", "c", [], [V("CI", 0, 1)], [lambda: g.iota(T.CI[:, 0:1], [[0, 1]], 0, 1)], 150.0)
    add("pool", "c", [], [V("JF", 0, 256)], [lambda: g.iota(T.JF[:, :], [[1, 256]], 0, 0, allow_small_or_imprecise_dtypes=True)], 600.0)
    add("pool", "c", [], [V("JK", 0, 256)], [lambda: g.iota(T.JK[:, :], [[0, 16], [1, 16]], 0, 0, allow_small_or_imprecise_dtypes=True)], 600.0)
    s = send([(T.cores[k], T.PLD[me], D(T.PST[k], "PST", k, k + 1), "ap", small(me)[k]) for k in others])
    arrive("ap", sum(len(small(r)[me]) for r in others), [D(None, "PLD", 0, 4)], s, 3000.0)
    runs = [(a, b) for a, b in ((0, me), (me + 1, 4)) if b > a]
    dma("sp", [(V("PI", 0, 256, 1, 32 * a, 32 * b), D(T.PLD[a:b], "PLD", a, b)) for a, b in runs], 98304)
    sf = {}
    if USE_HELPERS:
        s = send([(hp[(me, k)], T.FLD[me], D(T.FST[k], "FST", k, k + 1), "hf", fan_engines(T, topo, me)[k]) for k in others])
        for k in others:
            sf[(0, k)] = s
    for hf in ((1,) if USE_HELPERS else (0, 1)):
        for k in others:
            sf[(hf, k)] = send([(T.cores[k], T.FLD[4 * hf + me], D(T.FST[4 * hf + k], "FST", 4 * hf + k, 4 * hf + k + 1),
                                 "af%d" % (4 * hf + me), off_engines(me, k))])
    own = D(T.fr[32 * me:32 * me + 32, :], "fr", 0, 1)
    dma("sp", [(V("XW", 0, W, 1, 32 * me, 32 * me + 32), own), (V("XS", 0, W, 1, 32 * (me ^ 1), 32 * (me ^ 1) + 32), own)], 900000)
    for hf in (1, 0):
        for i, r in enumerate(reversed(others)):
            j = 4 * hf + r
            arrive("af%d" % j, len(off_engines(r, me)), [D(None, "FLD", j, j + 1)], sf[(hf, others[i])], 9000.0 if hf == 0 else 5000.0 + 2000 * i)
            src = D(T.FLD[j], "FLD", j, j + 1)
            dma("sp", [(V("XW", 2048 * hf, 2048 * hf + 2048, 1, 32 * r, 32 * r + 32), src),
                       (V("XS", 2048 * hf, 2048 * hf + 2048, 1, 32 * (r ^ 1), 32 * (r ^ 1) + 32), src)], 262144)

    CI = lambda i: V("CI", i, i + 1)
    J = lambda n: V("JF", 0, n)
    cp(C("p"), CI(0))
    ts(CI(1), CI(0), 15, None, Alu.bitwise_and)
    ts(CI(2), CI(0), 5, 1, Alu.logical_shift_right, Alu.bitwise_and)
    ts(CI(3), CI(0), 6, 1, Alu.logical_shift_right, Alu.bitwise_and)
    ts(CI(4), CI(0), 1, None, Alu.bitwise_and)
    ts(CI(5), CI(0), 14, None, Alu.bitwise_and)
    cp(C("k"), CI(1)); cp(C("b0"), CI(2)); cp(C("b1"), CI(3)); cp(C("odd"), CI(4))
    ts(C("s16"), C("k"), -1.0, C("p"), Alu.mult, Alu.add)
    ts(C("x1"), C("b0"), -64.0, 32.0, Alu.mult, Alu.add)
    ts(C("x2"), C("b1"), -128.0, 64.0, Alu.mult, Alu.add)
    ts(C("x3"), C("x1"), C("x2"), None, Alu.add)
    ts(C("t0"), C("s16"), 1.0, None, Alu.add)
    for x in (1, 2, 3):
        ts(C("t%d" % x), C("x%d" % x), C("s16"), 1.0 + 2 * x, Alu.add, Alu.add)
    UB = lambda x: V("UB", 144 * x, 144 * x + 144)
    for x in range(4):
        ts(UB(x), J(144), C("t%d" % x), None, Alu.is_equal)
    tt(UB(0), UB(0), UB(1), Alu.add); tt(UB(2), UB(2), UB(3), Alu.add); tt(UB(0), UB(0), UB(2), Alu.add)
    ts(V("M16", 0, 16), J(16), C("k"), None, Alu.is_equal)
    for k in range(16):
        if k % 2:
            act(V("UK", 144 * k, 144 * k + 144), UB(0), Act.Identity, V("M16", k, k + 1))
        else:
            ts(V("UK", 144 * k, 144 * k + 144), UB(0), V("M16", k, k + 1), None, Alu.mult, half=True)
    ts(M("P0"), J(128), C("p"), None, Alu.is_equal)
    for h in (1, 2):
        ts(C("u%d" % h), C("x%d" % h), C("p"), None, Alu.add)
        ts(M("P%d" % h), J(128), C("u%d" % h), None, Alu.is_equal)
    for x in range(4):
        ts(C("r%d" % x), CI(5), float(2 * x), None, Alu.is_equal)
    ts(C("u0"), C("s16"), 15.0, None, Alu.add)
    for x in range(3):
        ts(V("CW", 144 * x, 144 * x + 144), J(144), C("u0"), C("r%d" % x), Alu.is_equal, Alu.mult)
    fill(V("ONE", 0, 256), 1.0)
    fill(V("DW", 0, 16), 0.0)
    fill(C("cc"), 0.0)
    for nm, c in (("K0", 0.0), ("K2", 2.0), ("K3", 3.0), ("Kn", -1.0 / 128), ("K8", 0.125)):
        fill(M(nm), c)
    act(V("JB", 0, 256), J(256))
    ts(C("nl"), C("k"), 15.0, None, Alu.is_lt)
    ts(C("la"), C("k"), 15.0, None, Alu.is_equal)
    for h in (1, 2):
        ts(C("v%d" % (h - 1)), C("u%d" % h), 1.0, None, Alu.add)
        ts(M("S%d" % h), J(128), C("v%d" % (h - 1)), C("nl"), Alu.is_equal, Alu.mult)
        ts(C("v%d" % (h + 1)), C("u%d" % h), -15.0, None, Alu.add)
        ts(M("R%d" % h), J(128), C("v%d" % (h + 1)), C("la"), Alu.is_equal, Alu.mult)
        for nm in "PSR":
            act(M("%s%dd" % (nm, h)), M("%s%d" % (nm, h)), Act.Identity, 1.0 / 64)
    for nm, c in (("P0x64", 64.0), ("In63", -63.0), ("In64", -64.0), ("I4096", 4096.0), ("I16384", 16384.0), ("Ih", 0.5)):
        act(M(nm), M("P0"), Act.Identity, c)
    ts(C("sl"), C("s16"), 1.0 / 16, None, Alu.mult)
    ts(V("CS", 0, 8), J(8), C("sl"), 256.0, Alu.is_equal, Alu.mult)
    ts(V("CS", 8, 16), J(8), C("sl"), 256.0, Alu.is_equal, Alu.mult)
    ts(C("wt"), C("odd"), 63.0 / 64, 1.0 / 64, Alu.mult, Alu.add)
    ts(C("u3"), C("odd"), 8.0, C("sl"), Alu.mult, Alu.add)
    for x in (1, 2):
        ts(C("v%d" % (x + 3)), C("wt"), C("r%d" % x), None, Alu.mult)
        ts(V("CS", 16 * x, 16 * x + 16), J(16), C("u3"), C("v%d" % (x + 3)), Alu.is_equal, Alu.mult)
    ts(C("m0"), C("p"), 16.0, None, Alu.mult)
    ts(C("m1"), C("p"), 16.0, 2048.0, Alu.mult, Alu.add)
    OWN = [1, 3, 2]
    for t in range(3):
        h, hn = HS[t], (HS[t + 1] if t < 2 else 0)
        bit = C("b0" if h == 1 else "b1")
        if OWN[t] & h:
            ts(C("a%d" % t), bit, 1.0, None, Alu.mult)
        else:
            ts(C("a%d" % t), bit, -1.0, 1.0, Alu.mult, Alu.add)
        act(M("A%d" % t), M("P0"), Act.Identity, C("a%d" % t))
        ts(C("y%d" % t), C("a%d" % t), -16384.0, 16.0, Alu.mult, Alu.add)
        ts(C("y%d" % t), C("y%d" % t), C("k"), None, Alu.add)
        if hn:
            ts(C("cx"), C("x%d" % hn), 1.0 / 16, C("sl"), Alu.mult, Alu.add)
            ts(V("CS", 48 + 8 * t, 56 + 8 * t), J(8), C("cx"), C("r%d" % (h ^ hn)), Alu.is_equal, Alu.mult)
            ts(C("cx"), C("b1"), 64.0, C("x%d" % hn), Alu.mult, Alu.add)
            ts(C("t0"), C("b0"), 32.0, C("cx"), Alu.mult, Alu.add)
            ts(UB(1), J(144), C("t0"), 0.0, Alu.subtract, Alu.is_ge)
            ts(UB(2), J(144), C("t0"), 32.0, Alu.subtract, Alu.is_lt)
            tt(M("B%d" % hn), V("UB", 144, 272), V("UB", 288, 416), Alu.mult)
        else:
            ts(V("CS", 48 + 8 * t, 56 + 8 * t), J(8), C("sl"), C("r%d" % h), Alu.is_equal, Alu.mult)

    HI = lambda a, b: V("HL", 16 + a, 16 + b)
    LO = lambda a, b: V("HL", 288 + a, 288 + b)
    ts(V("XI", 0, 256), V("PI", 0, 256), 4032, None, Alu.bitwise_and)
    ts(V("XI", 256, 512), V("PI", 0, 256), 63, None, Alu.bitwise_and)
    cp(HI(0, 256), V("XI", 0, 256)); cp(LO(0, 256), V("XI", 256, 512))
    cp(V("HL", 15, 288, 272), V("XI", 255, 512, 256))
    cp(V("XW", W, W + 16), V("XW", 0, 16))

    def wrap(bank, src, x, lo, hi):
        mm([(PS(bank, lo // 16, hi // 16), V("CW", 144 * x + 15 - k, 144 * x + 143 - k), V(src, lo + k, hi, 16), k == 0, k == 15)
            for k in range(16)])

    def across(out, src, base, bh, rhs, stop):
        mm([(out(k), V(src, base + 2048 * bh + k, base + 2048 * bh + 2048, 16), rhs, False, stop and k == 15) for k in range(16)])

    def pointers(t):
        hn = HS[t + 1] if t < 2 else 0
        P = M("P%d" % hn)
        for a, e in (((0, 256),) if t < 0 else ((0, 128), (128, 256))):
            lb = 6 if e == 128 else 7
            mm([(PS(lb, a, e), P, HI(a, e), True, False), (PS(lb, a, e), P, LO(a, e), False, True)])
            cp(V("LM", a, e), PS(lb, a, e))
            if t == 2:
                act(V("YP", a, e), PS(lb, a, e))
            for j in range(8):
                if e == 128:
                    o = lambda k: PS((0, 2, 7, 0)[j // 2], (k % 4) * 128, (k % 4 + 1) * 128)
                else:
                    o = lambda k: PS((1, 3, 2, 0)[j % 4], (k % 2) * (e - a), (k % 2 + 1) * (e - a))
                mm([(o(k), V("UK", 144 * k + 1 - lo, 144 * k + 129 - lo), (HI, LO)[lo](a, e), lo == 0, lo == 1) for k in (2 * j, 2 * j + 1) for lo in (0, 1)])
                for k in (2 * j, 2 * j + 1):
                    copy(PE0[j % 2] if e == 128 else ("act" if j % 2 else "dve"), V("PW", 16 * a + k, 16 * e, 16), o(k))
        if t == 2:
            dma("sp", [(D(T.QST[:], "QST", 0, 4), V("YP", 0, 256)),
                       (D(T.yp[32 * me:32 * me + 32, :], "yp", me, me + 1), V("YP", 0, 256, 1, 32 * (me ^ 2), 32 * (me ^ 2) + 32))], 131072)
            s = send([(T.cores[k], T.QLD[me], D(T.QST[k ^ 2], "QST", k ^ 2, (k ^ 2) + 1), "ay", small(me)[k]) for k in others])
            arrive("ay", sum(len(small(r)[me]) for r in others), [D(None, "QLD", 0, 4)], s, 11000.0)
            dma("act", [(D(T.yp[32 * a:32 * b, :], "yp", a, b), D(T.QLD[a:b], "QLD", a, b)) for a, b in runs], 98304)
        for c in range(4):
            gather("dve" if c % 2 else "act", V("GA", 1024 * c, 1024 * c + 1024), V("PW", 0, W), "LM", 1024 * c, 1024 * c + 1024)
        if t >= 0:
            for bh in range(2):
                a, e = 128 * bh, 128 * bh + 128
                mm([(PS(6 + bh, 0, 128), M("Kn"), V("JK", 0, 128), True, False)])
                across(lambda k: PS(6 + bh, k, 128, 16), "GA", 0, bh, V("CS", 48 + 8 * t, 56 + 8 * t), True)
                ts(V("CON", a, e), PS(6 + bh, 0, 128), C("m%d" % bh), None, Alu.is_equal)
                o = PS(2 + bh, 0, 128)
                mm([(o, M("K8"), V("JB", a, e), True, False), (o, V("TB", 384 * bh + 256, 384 * bh + 384), M("I4096"), False, False)])
                mm([(o, V("CON", a, e), M("I16384"), False, True)])
                ts(V("LY", a, e), o, C("y%d" % t), 0.0, Alu.add, Alu.max)
            if t < 2:
                cn = "CN%d" % t
                mm([(PS(4, 0, 1), V("CON", 128 * bh, 128 * bh + 128), V("ONE", 0, 1), bh == 0, bh == 1) for bh in range(2)])
                act(V(cn, 8 * me, 8 * me + 1), PS(4, 0, 1))
                s = send([(T.cores[k], T[cn][:, 8 * me:8 * me + 1], V(cn, 8 * me, 8 * me + 1), "ac%d" % t, small(me)[k]) for k in others])
                arrive("ac%d" % t, sum(len(small(r)[me]) for r in others), [V(cn, 8 * r, 8 * r + 1) for r in others], s, 4000.0)
        if t < 2:
            for c in range(4):
                wrap(5, "GA", 0, 1024 * c, 1024 * c + 1024)
            cp(V("LU", 0, 256), PS(5, 0, 256))
        if t >= 0:
            lift(t, hn)
        if t < 2:
            for c in range(4):
                gather(BE[t + 1][c], V("GB", 1024 * c, 1024 * c + 1024), V("PW", 0, W), "LU", 1024 * c, 1024 * c + 1024)
                chain()
                wrap(4, "GB", hn, 1024 * c, 1024 * c + 1024)
            cp(V("L1", 0, 256), PS(4, 0, 256))
            if t >= 0:
                cn = "CN%d" % t
                mm([(PS(6, 0, 4), M("B%d" % hn), V(cn, 0, 32, 8), True, True)])
                add("dve", "c", [PS(6, 0, 4)], [C("cx")], [lambda: g.vector.tensor_reduce(C("cx")[0], PS(6, 0, 4)[0], Ax.X, Alu.add)], 120.0)
                ts(CI(6), C("cx"), -1.5, 0.25, Alu.add, Alu.mult)
                ts(C("cc"), CI(6), -4.0, C("cx"), Alu.mult, Alu.add)
            S, R = M("S%d" % hn), M("R%d" % hn)
            o = PS(7, 0, 256)
            mm([(o, S, HI(0, 256), True, False), (o, S, LO(0, 256), False, False), (o, R, HI(-1, 255), False, False), (o, R, LO(-1, 255), False, True)])
            ts(V("L3", 0, 256), o, C("cc"), 1.0, Alu.add, Alu.add)
            ts(V("FL", 0, 256), o, C("cc"), 4095.0, Alu.add, Alu.is_ge)
            act(M("CDG"), M("P0"), Act.Identity, C("cc"))
            for c in range(4):
                gather(CE[t + 1][c], V("GC", 1024 * c, 1024 * c + 1024), V("GB", 0, W), "LU", 1024 * c, 1024 * c + 1024)
                wrap(6, "GC", hn, 1024 * c, 1024 * c + 1024)
            cp(V("L2", 0, 256), PS(6, 0, 256))

    def lift(t, hn):
        for c in range(4):
            lo = 1024 * c
            gather(YE[t][c], V("YG", lo, lo + 1024), V("DW", 0, 16 + 8 * W), "LY", lo, lo + 1024)
            chain()
        for c in range(4):
            lo = 1024 * c
            b = 2 * (c % 2)
            for i in range(2):
                a = lo + 512 * i
                mm([(PS(b + i, 0, 512), M("A%d" % t), V("XS", a, a + 512), True, False), (PS(b + i, 0, 512), M("Ih"), V("YG", a, a + 512), False, True)])
            act(V("SF", lo, lo + 1024), PS(b, 0, 1024), Act.Abs, 1.0 - 2.0 ** -11)
            chain()
            ts(V("XW", lo, lo + 1024), V("SF", lo, lo + 1024), MAGIC, MAGIC, Alu.add, Alu.subtract)
            chain()
            if t < 2:
                if c == 0:
                    ts(V("XW", W, W + 16), V("SF", 0, 16), MAGIC, MAGIC, Alu.add, Alu.subtract)
                n = 32 * hn
                dma("sp", [(V("XS", lo, lo + 1024, 1, p ^ n, (p ^ n) + n), V("XW", lo, lo + 1024, 1, p, p + n)) for p in range(0, 128, n)], 262144)
            else:
                o = 32 * (me ^ 2)
                dma("sp", [(D(T.OST[4 * c:4 * c + 4], "OST", 4 * c, 4 * c + 4), V("XW", lo, lo + 1024))], 262144)
                dma("sp", [(D(T.yf[32 * me:32 * me + 32, lo:lo + 1024], "yf", 4 * c + me, 4 * c + me + 1), V("XW", lo, lo + 1024, 1, o, o + 32))], 65536)
                src = lambda k: D(T.OST[4 * c + (k ^ 2)], "OST", 4 * c + (k ^ 2), 4 * c + (k ^ 2) + 1)
                if USE_HELPERS and c % 2 == 0:
                    s = send([(hp[(me, k)], T.OLD[4 * c + me], src(k), "ho%d" % c, fan_engines(T, topo, me)[k]) for k in others])
                else:
                    for k in others:
                        s = send([(T.cores[k], T.OLD[4 * c + me], src(k), "ao%d" % c, off_engines(me, k))])
                arrive("ao%d" % c, sum(len(off_engines(r, me)) for r in others), [D(None, "OLD", 4 * c, 4 * c + 4)], s, 8000.0)
                dma("act", [(D(T.yf[32 * a:32 * b, lo:lo + 1024], "yf", 4 * c + a, 4 * c + b), D(T.OLD[4 * c + a:4 * c + b], "OLD", 4 * c + a, 4 * c + b))
                            for a, b in runs], 196608)

    def choose(t):
        h = HS[t]
        done = [0, 0]
        for k, bh in ORDER:
            i = done[bh]
            done[bh] += 1
            lst = ("LM", "L1", "L2", "L3")[k]
            b = 2 * (i % 2) + bh
            H, L = PS(b, 0, 128), PS(b, 128, 256)
            a, e = 128 * bh, 128 * bh + 128
            it = [(PS(b, 0, 256), V("ONE", 0, 128) if k == 1 else M("K%d" % k), V("ONE", 0, 256), True, False)]
            if k == 0:
                it += [(H, HI(a, e), M("P%dd" % h), False, False), (L, LO(a, e), M("P%d" % h), False, False)]
            if k == 3:
                fl = V("FL", a, e)
                it += [(H, HI(a, e), M("S%dd" % h), False, False), (H, HI(a - 1, e - 1), M("R%dd" % h), False, False),
                       (L, LO(a, e), M("S%d" % h), False, False), (L, LO(a - 1, e - 1), M("R%d" % h), False, False),
                       (L, V("ONE", 0, 128), M("P0"), False, False), (L, V("ONE", 0, 128), M("CDG"), False, False),
                       (H, fl, M("In63"), False, False), (L, fl, M("In64"), False, False)]
            mm(it)
            if k in (1, 2):
                across(lambda j: PS(b, j, 256, 16), "GB" if k == 1 else "GC", 0, bh, V("CS", 16 * h, 16 * h + 16), False)
            lo = 2048 * bh
            for n in (DLAST if (k, bh) == ORDER[-1] else DCH):
                d = V("DW", 16 + W * k + lo, 16 + W * k + lo + n)
                gather("dve", d, V("XW", 0, W + 16), lst, lo, lo + n, V("XS", lo, lo + n))
                chain()
                act(V("DW", A2 + W * k + lo, A2 + W * k + lo + n), d, Act.Abs, 2.0)
                lo += n
            across(lambda j: PS(b, j, 256, 16), "DW", A2 + W * k, bh, V("CS", 0, 16), True)
            kf = V("KF", 256 * bh, 256 * bh + 256)
            if i == 0:
                copy(KE, kf, PS(b, 0, 256))
            else:
                tt(V("KI", 256 * bh, 256 * bh + 256) if i == 3 else kf, kf, PS(b, 0, 256), Alu.min)
        for bh in range(2):
            x, a, e = 384 * bh, 128 * bh, 128 * bh + 128
            ts(V("XI", x, x + 256), V("KI", 256 * bh, 256 * bh + 256), 127, None, Alu.bitwise_and)
            cp(V("TB", x, x + 256), V("XI", x, x + 256))
            mm([(PS(4, a, e), V("TB", x, x + 128), M("P0x64"), True, True), (PS(5, a, e), V("TB", x + 128, x + 256), M("P0"), True, True)])
            act(HI(a, e), PS(4, a, e))
            copy("dve" if bh else "act", LO(a, e), PS(5, a, e))
            ts(V("XI", x + 256, x + 384), V("KI", 256 * bh, 256 * bh + 128), 7, 3, Alu.logical_shift_right, Alu.bitwise_and)
            cp(V("TB", x + 256, x + 384), V("XI", x + 256, x + 384))
        if t < 2:
            act(V("HL", 15, 288, 272), V("HL", 271, 544, 272))
            ops[-1]["w"] = [HI(-1, 0)[1:], LO(-1, 0)[1:]]
            ops[-1]["r"] = [HI(255, 256)[1:], LO(255, 256)[1:]]

    pointers(-1)
    for t in range(3):
        choose(t)
        pointers(t)
    emit(g, T, ops, nsent[0])


def emit(g, T, ops, nsent):
    n = len(ops)
    seen = {}
    for i, o in enumerate(ops):
        deps = {}
        acc = {}
        for mode, regs in ((0, o["r"]), (1, o["w"])):
            for name, lo, hi, p0, p1, st in regs:
                if name == "PS":
                    lo, hi, p0, p1, st = lo // 512, (hi + 511) // 512, 0, 128, 1
                acc[(name, lo, hi, p0, p1, mode, st)] = 1
        for name, lo, hi, p0, p1, mode, st in acc:
            for j, l2, h2, q0, q1, m2, s2 in seen.get(name, []):
                if l2 < hi and lo < h2 and q0 < p1 and p0 < q1 and not (st == s2 and (lo - l2) % st):
                    same = ops[j]["eng"] == o["eng"] and ops[j]["kind"] == "c" and o["kind"] == "c"
                    if mode or m2 or (name == "PS" and not same):
                        need = (not same) or name != "PS"
                        deps[j] = deps.get(j, False) or need
        for name, lo, hi, p0, p1, mode, st in acc:
            lst = seen.setdefault(name, [])
            if mode and st == 1:
                lst[:] = [x for x in lst if not (lo <= x[1] and x[2] <= hi and p0 <= x[3] and x[4] <= p1)]
        for name, lo, hi, p0, p1, mode, st in acc:
            seen[name].append((i, lo, hi, p0, p1, mode, st))
        if o["after"] is not None:
            deps = {o["after"]: False}
        if o.get("behind") is not None:
            deps.setdefault(o["behind"], False)
        o["deps"] = deps
    users = [[] for _ in range(n)]
    for i, o in enumerate(ops):
        for j in o["deps"]:
            users[j].append(i)

    def timeline(prio, slack):
        left = [len(o["deps"]) for o in ops]
        ready = {i: 0.0 for i in range(n) if left[i] == 0}
        free, order, t0, t1 = {}, [], [0.0] * n, [0.0] * n
        while ready:
            first = {}
            for i, rt in ready.items():
                e = ops[i]["eng"]
                s = max(rt, free.get(e, 0.0))
                if e not in first or s < first[e]:
                    first[e] = s
            e = min(first, key=lambda x: first[x])
            i = max((i for i, rt in ready.items() if ops[i]["eng"] == e and rt <= first[e] + slack), key=lambda i: (prio[i], -i))
            o = ops[i]
            st = max(ready.pop(i), first[e])
            order.append(i)
            if e:
                free[e] = st + o["busy"]
            t0[i], t1[i] = st, st + o["busy"] + o["lat"]
            for u in users[i]:
                left[u] -= 1
                if left[u] == 0:
                    ready[u] = max(t1[j] + HOP if need or ops[u]["kind"] == "a" else t0[j] for j, need in ops[u]["deps"].items())
        return order, t0, t1

    def backwards(prio, slack):
        left = [len(u) for u in users]
        ready = {i: ops[i]["lat"] for i in range(n) if left[i] == 0}
        free, end = {}, [0.0] * n
        while ready:
            first = {}
            for i, rt in ready.items():
                e = ops[i]["eng"]
                s = max(rt, free.get(e, 0.0))
                if e not in first or s < first[e]:
                    first[e] = s
            e = min(first, key=lambda x: first[x])
            i = max((i for i, rt in ready.items() if ops[i]["eng"] == e and rt <= first[e] + slack), key=lambda i: (prio[i], i))
            end[i] = max(ready.pop(i), first[e]) + ops[i]["busy"]
            if e:
                free[e] = end[i]
            for j in ops[i]["deps"]:
                left[j] -= 1
                if left[j] == 0:
                    ready[j] = max(end[u] + (HOP if ops[u]["deps"][j] else 0.0) for u in users[j]) + ops[j]["lat"]
        return end

    def replay(order, gath, pe, hop):
        free, t0, t1 = {}, [0.0] * n, [0.0] * n
        for i in order:
            o = ops[i]
            b = 60 + CYC * gath * o["gn"] if "gn" in o else o["busy"] * (pe if o["eng"] == "pe" else 1.0)
            s = max([free.get(o["eng"], 0.0)] + [t1[j] + hop if need or o["kind"] == "a" else t0[j] for j, need in o["deps"].items()])
            t0[i], t1[i] = s, s + b + o["lat"]
            if o["eng"]:
                free[o["eng"]] = s + b
        return max(t1)

    def worth(order):
        return sum(replay(order, a, b, c) / w for a, b, c, w in ((1.2, 1.0, 120.0, 0.87), (GATH, 1.0, 120.0, 1.0), (1.9, 1.0, 120.0, 1.13), (GATH, 1.0, 300.0, 1.1)))

    base = [0.0] * n
    for i in range(n - 1, -1, -1):
        base[i] += ops[i]["busy"] + ops[i]["lat"] + HOP
        for j in ops[i]["deps"]:
            base[j] = max(base[j], base[i])
    for i, o in enumerate(ops):
        if o["eng"] in ("dve", "act") and o["busy"] < 500:
            base[i] += BOOST
    rng = np.random.RandomState(1)
    prio, best = base, None
    for k in range(TRIES):
        if best is None:
            cand, slack = base, SLACK
        else:
            src = t1 if k % 4 else best[3]
            cand = backwards([x + NOISE * float(rng.rand()) for x in src], float(rng.choice([0.0, 150.0])))
            slack = float(rng.choice([0.0, 150.0, 300.0, 600.0]))
        order, t0, t1 = timeline(cand, slack)
        w = worth(order)
        if best is None or w < best[0]:
            best, prio = (w, order, t0, t1), cand
    order = best[1]
    for p, i in enumerate(order):
        ops[i]["pos"], ops[i]["t0"], ops[i]["t1"] = p, best[2][i], best[3][i]
    queue = {"dve": g.vector, "act": g.scalar, "pe": g.tensor, "pool": g, "sp": g.sync}
    count = {}
    waited = {}
    nd = 0
    for i in order:
        o = ops[i]
        if o["kind"] == "a":
            o["tok"] = o["sem"]
            count[o["sem"][0]] = o["sem"][1]
            continue
        e = o["eng"]
        want = {}
        for j, need in o["deps"].items():
            if need:
                s, v = ops[j]["tok"]
                want[s] = max(want.get(s, 0), v)
        for s, v in want.items():
            if waited.get((e, s), 0) < v:
                queue[e].wait_ge(T.sem[s], v)
                waited[(e, s)] = v
        if o["kind"] == "r":
            o["fns"][0]()
            continue
        if o["kind"] == "d":
            s, inc = "d%d" % nd, 16
            nd += 1
        else:
            s, inc = e, 1
        for f in o["fns"]:
            f().then_inc(T.sem[s], inc)
            count[s] = count.get(s, 0) + inc
        o["tok"] = (s, count[s])
    g.wait_ge(T.sem.sent, nsent)
    for s, v in count.items():
        g.wait_ge(T.sem[s], v)
    return ops
